import numpy as np
import ml_dtypes


def mxq(x, axis, fmt="e4m3"):
    dtype, down = {"e4m3": (ml_dtypes.float8_e4m3fn, 7), "e5m2": (ml_dtypes.float8_e5m2, 14)}[fmt]
    v = np.moveaxis(np.asarray(x, np.float32).astype(ml_dtypes.bfloat16).astype(np.float64), axis, -1)
    blocks = v.reshape(v.shape[:-1] + (-1, 32))
    amax = np.abs(blocks).max(-1, keepdims=True)
    byte = np.maximum(np.where(amax > 0, np.frexp(amax)[1] - 1 + 127, 0) - down, 1)
    scale = np.exp2(byte - 127.0)
    codes = (blocks / scale).astype(np.float32).astype(dtype).astype(np.float64)
    return np.moveaxis((codes * scale).reshape(v.shape), -1, axis)


WIDE = False


def mx_kscale(k):
    if not WIDE:
        return np.ones(k)
    levels = np.array([10, -10, 5, -5, 0])
    if k % 512:
        return np.exp2(np.random.permutation(np.resize(levels, k // 32))).repeat(32)
    a = np.empty((k // 512, 16))
    for p in range(k // 512):
        a[p, :8] = np.random.permutation(np.resize(levels, 8))
        for g in range(8):
            far = levels[np.abs(levels - a[p, g]) >= 10]
            a[p, g + 8] = far[np.random.randint(len(far))]
    return np.exp2(a.ravel()).repeat(32)


def f64(x):
    return np.asarray(x).astype(np.float64)


def striped(idx):
    return np.tile(np.asarray(idx).reshape(-1, 16).T, (8, 1)).astype(np.uint16)


def unstriped(offs):
    return offs[:16].T.reshape(-1).astype(np.int64)


E2M1 = np.array([0.0, 0.5, 1.0, 1.5, 2.0, 3.0, 4.0, 6.0, -0.0, -0.5, -1.0, -1.5, -2.0, -3.0, -4.0, -6.0])


def pack_weight(w, fmt):
    k, n = w.shape
    w = f64(np.asarray(w, np.float32).astype(ml_dtypes.bfloat16)).reshape(k // 32, 32, n)
    amax = np.abs(w).max(1)
    if fmt == "e4m3":
        byte = np.frexp(amax)[1] - 1 + 127 - 7
    else:
        mant, ex = np.frexp(amax / 6.0)
        byte = np.where(mant > 0.5, ex, ex - 1) + 127
    byte = np.clip(np.where(amax > 0, byte, 1), 1, 254)
    scaled = (w * np.exp2(127.0 - byte)[:, None, :]).reshape(k, n).astype(np.float32)
    by_word = np.ascontiguousarray(scaled.reshape(k // 512, 128, 4, n).transpose(0, 1, 3, 2))
    if fmt == "e4m3":
        words = by_word.astype(ml_dtypes.float8_e4m3fn).view(np.uint8)
    else:
        c = by_word.astype(ml_dtypes.float4_e2m1fn).view(np.uint8) & 0xF
        words = (c[..., 0::2] | (c[..., 1::2] << 4)).reshape(k // 512, 128, 2 * n)
    return np.ascontiguousarray(words), np.ascontiguousarray(byte.astype(np.uint8).reshape(k // 512, 16, n))


def unpack_weight(words, scales, fmt):
    g, _, n = scales.shape
    words = np.ascontiguousarray(words).reshape(g, 128, n, -1)
    if fmt == "e4m3":
        vals = words.view(ml_dtypes.float8_e4m3fn).astype(np.float64)
    else:
        nib = np.empty((g, 128, n, 4), np.uint8)
        nib[..., 0::2] = words & 0xF
        nib[..., 1::2] = words >> 4
        vals = E2M1[nib]
    vals = vals * np.repeat(np.exp2(scales.astype(np.float64) - 127.0), 8, axis=1)[..., None]
    return vals.transpose(0, 1, 3, 2).reshape(g * 512, n)


def bf(x):
    return np.asarray(x, np.float32).astype(ml_dtypes.bfloat16)


def planes(Y):
    r, m = Y.shape
    b = f64(bf(Y)).reshape(r // 32, 32, m)
    amax = np.abs(b).max(1)
    byte = np.clip(np.where(amax > 0, np.frexp(amax)[1] - 1 + 127 - 7, 1), 1, 254)
    codes = (b * np.exp2(127.0 - byte)[:, None, :]).reshape(r, m).astype(np.float32).astype(ml_dtypes.float8_e4m3fn).view(np.uint8)
    words = codes.reshape(r // 512, 128, 4, m).transpose(0, 1, 3, 2)
    return np.ascontiguousarray(words), np.ascontiguousarray(byte.astype(np.uint8).reshape(r // 512, 16, m))


K, T, J, I, S, R, N = 1024, 2048, 1024, 512, 512, 512, 512


def setup_inputs():
    n = np.random.standard_normal
    idx = np.random.permutation(T)[:J]
    idx2 = np.random.permutation(J)[:I]
    idx3 = np.random.permutation(J)[:S]
    fk = mx_kscale(K)
    fr = mx_kscale(R)
    xqp = pack_weight(n((K, T)) / fk[:, None], "e2m1")
    wap = pack_weight(n((K, R)) * 1 / np.sqrt(K) * fk[:, None] * fr, "e4m3")
    dap = pack_weight(n((R, N)) * 1 / np.sqrt(R) / fr[:, None], "e2m1")
    dbp = pack_weight(n((R, N)) * 1 / np.sqrt(R) / fr[:, None], "e4m3")
    return {
        "xq_words": xqp[0],
        "xq_scales": xqp[1],
        "wa_words": wap[0],
        "wa_scales": wap[1],
        "da_words": dap[0],
        "da_scales": dap[1],
        "db_words": dbp[0],
        "db_scales": dbp[1],
        "offs": striped(idx),
        "offs2": striped(idx2),
        "offs3": striped(idx3),
    }


def reference(xq_words, xq_scales, wa_words, wa_scales, da_words, da_scales, db_words, db_scales, offs, offs2, offs3):
    idx = unstriped(offs)
    idx2 = unstriped(offs2)
    idx3 = unstriped(offs3)
    xqu = unpack_weight(xq_words, xq_scales, "e2m1")
    wau = unpack_weight(wa_words, wa_scales, "e4m3")
    dau = unpack_weight(da_words, da_scales, "e2m1")
    dbu = unpack_weight(db_words, db_scales, "e4m3")
    xqidxg = xqu[:, idx]
    a = wau.T @ xqidxg
    hid = np.maximum(a, 0.0)
    hididx2q = mxq(hid[:, idx2], 0, "e4m3")
    p = dau.T @ hididx2q
    hididx3q = mxq(hid[:, idx3], 0, "e4m3")
    q = dbu.T @ hididx3q
    pg = np.zeros((N, J))
    pg[:, idx2] = p
    qg = np.zeros((N, J))
    qg[:, idx3] = q
    y = pg + qg
    words, scales = planes(y)
    return y, words, scales

@@ -1,0 +1,258 @@
+from contextlib import ExitStack
+
+import concourse.mybir as mybir
+
+K, T, J, I, S, R, N = 1024, 2048, 1024, 512, 512, 512, 512
+FLOPS = 2 * K * R * J + 2 * R * N * I + 2 * R * N * S
+
+F32 = mybir.dt.float32
+BF16 = mybir.dt.bfloat16
+I32 = mybir.dt.int32
+U32 = mybir.dt.uint32
+U16 = mybir.dt.uint16
+U8 = mybir.dt.uint8
+FP8X4 = mybir.dt.float8_e4m3fn_x4
+FP4X4 = mybir.dt.float4_e2m1fn_x4
+RELU = mybir.ActivationFunctionType.Relu
+ADD = mybir.AluOpType.add
+
+P = 128
+PACK = 4
+BANK = 512
+PASSES = K // (P * PACK)
+HALVES = J // BANK
+
+
+def tile_list_expert_down_two_roads_pl_kernel(
+    tc, xq_words, xq_scales, wa_words, wa_scales, da_words, da_scales, db_words, db_scales,
+    offs, offs2, offs3, out_0, out_1, out_2,
+):
+    nc = tc.nc
+    with ExitStack() as ctx:
+        lists = ctx.enter_context(tc.tile_pool(name="lists", bufs=1))
+        sb = ctx.enter_context(tc.tile_pool(name="sb", bufs=1))
+        psum = ctx.enter_context(tc.psum_pool(name="psum", bufs=1))
+
+        def tile(name, cols, dtype):
+            return sb.tile([P, cols], dtype, name=name, align_bytes=64)
+
+        def bank(b):
+            return psum.tile([P, BANK], F32, name="bank%d" % b)
+
+        list1 = lists.tile([P, J // 16], U16, name="list1")
+        list2 = lists.tile([P, I // 16], U16, name="list2")
+        list3 = lists.tile([P, S // 16], U16, name="list3")
+
+        xs_rows = sb.tile([P, T], U8, name="xs_rows", tag="xs_rows", align_bytes=64)
+        xs_picked = tile("xs_picked", J, U8)
+        xs = tile("xs", PASSES * J, U8)
+        xw = [tile("xw%d" % z, T, U16) for z in range(PASSES)]
+        wa_raw = tile("wa_raw", PASSES * R, I32)
+        was_raw = tile("was_raw", PASSES * R, U8)
+        da_raw = tile("da_raw", 2 * N, U8)
+        db_raw = tile("db_raw", N, I32)
+        p_pages = [tile("p_page%d" % u, J, F32) for u in range(2)]
+        q_page = tile("q_page", J, F32)
+
+        nc.sync.dma_start(list1[:], offs)
+        nc.sync.dma_start(
+            xs_rows[0:32, :].bitcast(I32), xq_scales.rearrange("z q c -> (z q) c").bitcast(I32)
+        )
+        for z in range(PASSES):
+            nc.sync.dma_start(xw[z][:].bitcast(I32), xq_words[z].bitcast(I32))
+        nc.sync.dma_start(
+            wa_raw[:].rearrange("p (z c) -> p z c", z=PASSES),
+            wa_words.rearrange("z p c r -> p z (c r)").bitcast(I32),
+        )
+        nc.vector.memset(xs_rows[32:64, :].bitcast(I32), 0)
+        nc.vector.memset(xs_rows[64:128, :].bitcast(I32), 0)
+        nc.vector.memset(was_raw[:].bitcast(I32), 0)
+        nc.vector.memset(xs[:].bitcast(I32), 0)
+        for q in range(4):
+            nc.sync.dma_start(
+                was_raw[32 * q : 32 * q + 4, :].bitcast(I32).rearrange("r (z c) -> r z c", z=PASSES),
+                wa_scales[:, 4 * q : 4 * q + 4, :].bitcast(I32).rearrange("z r c -> r z c"),
+            )
+        nc.sync.dma_start(list2[:], offs2)
+        nc.sync.dma_start(list3[:], offs3)
+        nc.sync.dma_start(da_raw[:].bitcast(I32), da_words[0].bitcast(I32))
+        nc.sync.dma_start(db_raw[:], db_words[0].rearrange("p c r -> p (c r)").bitcast(I32))
+        for page in p_pages + [q_page]:
+            nc.vector.memset(page[:], 0.0)
+
+        nc.vector.tensor_copy(xs_picked[:], xs_rows[:].indirect(list1[:]))
+        for z in range(PASSES):
+            for q in range(4):
+                row = 16 * z + 4 * q
+                (nc.scalar if q % 2 else nc.sync).dma_start(
+                    xs[32 * q : 32 * q + 4, z * J : (z + 1) * J].bitcast(I32),
+                    xs_picked[row : row + 4, :].bitcast(I32),
+                )
+
+        ds_raw = sb.tile([P, N], U8, name="ds_raw", tag="xs_rows", align_bytes=64)
+        nc.vector.memset(ds_raw[:].bitcast(I32), 0)
+        for q in range(4):
+            nc.sync.dma_start(
+                ds_raw[32 * q : 32 * q + 4, :].bitcast(I32), da_scales[0, 4 * q : 4 * q + 4, :].bitcast(I32)
+            )
+            nc.sync.dma_start(
+                ds_raw[32 * q + 4 : 32 * q + 8, :].bitcast(I32), db_scales[0, 4 * q : 4 * q + 4, :].bitcast(I32)
+            )
+
+        wa = tile("wa", PASSES * R, I32)
+        was = tile("was", PASSES * R, U8)
+        hid = tile("hid", PACK * J, F32)
+        xg = {}
+
+        def pick_words(h):
+            for z in range(PASSES):
+                xg[(z, h)] = tile("xg%d%d" % (z, h), BANK, U16)
+                cols = slice(h * BANK // 16, (h + 1) * BANK // 16)
+                nc.vector.tensor_copy(xg[(z, h)][:], xw[z][:].indirect(list1[:, cols]))
+
+        def hidden(h):
+            banks = [bank(PACK * h + t) for t in range(PACK)]
+            for z in range(PASSES):
+                for t in range(PACK):
+                    cols = slice(z * R + t * P, z * R + (t + 1) * P)
+                    nc.tensor.matmul_mx(
+                        out=banks[t][:],
+                        lhsT=wa[:, cols].bitcast(FP8X4),
+                        lhsT_scale=was[:, cols],
+                        rhs=xg[(z, h)][:].bitcast(FP4X4),
+                        rhs_scale=xs[:, z * J + h * BANK : z * J + (h + 1) * BANK],
+                        start=(z == 0),
+                        stop=(z == PASSES - 1),
+                    )
+            for t in range(PACK):
+                nc.scalar.activation(hid[:, t * J + h * BANK : t * J + (h + 1) * BANK], banks[t][:], RELU)
+
+        pick_words(0)
+        nc.vector.tensor_copy(
+            wa[:].rearrange("p (z t c i) -> p z c t i", z=PASSES, t=PACK, i=4),
+            wa_raw[:].rearrange("p (z c i t) -> p z c t i", z=PASSES, t=PACK, i=4),
+        )
+        nc.vector.tensor_copy(
+            was[:].rearrange("p (z t m) -> p z t m", z=PASSES, t=PACK),
+            was_raw[:].rearrange("p (z m t) -> p z t m", z=PASSES, t=PACK),
+        )
+        hidden(0)
+        pick_words(1)
+        hidden(1)
+
+        da = tile("da", 2 * N, U8)
+        db = tile("db", N, I32)
+        ds = tile("ds", N, U8)
+        nc.vector.tensor_copy(
+            da[:].rearrange("p (t m b) -> p t m b", t=PACK, b=2),
+            da_raw[:].rearrange("p (m t b) -> p t m b", t=PACK, b=2),
+        )
+        nc.vector.tensor_copy(
+            ds[:].rearrange("p (t m) -> p t m", t=PACK), ds_raw[:].rearrange("p (m t) -> p t m", t=PACK)
+        )
+        nc.vector.tensor_copy(
+            db[:].rearrange("p (t c i) -> p c t i", t=PACK, i=4),
+            db_raw[:].rearrange("p (c i t) -> p c t i", t=PACK, i=4),
+        )
+
+        picked_a = tile("picked_a", PACK * I, F32)
+        work = tile("work", PACK * S, F32)
+        rounded_a = work[:, 2 * S : 4 * S].bitcast(BF16)
+        rounded_b = tile("rounded_b", PACK * S, BF16)
+        codes = [tile("codes%d" % u, BANK, U32) for u in range(2)]
+        scales = [tile("scales%d" % u, BANK, U8) for u in range(2)]
+        staged = tile("staged", 5 * BANK, F32)
+
+        def interleave(dst, src):
+            nc.scalar.copy(
+                dst.rearrange("p (c i t) -> p c t i", t=PACK, i=4),
+                src.rearrange("p (t c i) -> p c t i", t=PACK, i=4),
+            )
+
+        for t in range(PACK):
+            nc.vector.tensor_copy(
+                picked_a[:, t * I : (t + 1) * I], hid[:, t * J : (t + 1) * J].indirect(list2[:])
+            )
+        interleave(rounded_a, picked_a[:])
+        for t in range(2):
+            nc.vector.tensor_copy(work[:, t * S : (t + 1) * S], hid[:, t * J :].indirect(list3[:]))
+        nc.vector.quantize_mx(out=codes[0][:].bitcast(FP8X4), scales=scales[0][:], in_=rounded_a)
+        for t in range(2, PACK):
+            nc.vector.tensor_copy(work[:, t * S : (t + 1) * S], hid[:, t * J :].indirect(list3[:]))
+
+        p_src = [staged[:, 0:BANK]] + [work[:, u * BANK : (u + 1) * BANK] for u in range(3)]
+        q_src = [staged[:, (u + 1) * BANK : (u + 2) * BANK] for u in range(PACK)]
+        p_banks = [bank(t) for t in range(PACK)]
+        for t in range(PACK):
+            nc.tensor.matmul_mx(
+                out=p_banks[t][:],
+                lhsT=da[:, 2 * t * P : 2 * (t + 1) * P].bitcast(FP4X4),
+                lhsT_scale=ds[:, t * P : (t + 1) * P],
+                rhs=codes[0][:].bitcast(FP8X4),
+                rhs_scale=scales[0][:],
+                start=True,
+                stop=True,
+            )
+        nc.scalar.copy(p_src[0], p_banks[0][:])
+        interleave(rounded_b[:], work[:])
+        nc.vector.tensor_copy(p_pages[0][:].indirect(list2[:]), p_src[0])
+        nc.vector.quantize_mx(out=codes[1][:].bitcast(FP8X4), scales=scales[1][:], in_=rounded_b[:])
+        q_banks = [bank(PACK + t) for t in range(PACK)]
+        for t in range(PACK):
+            nc.tensor.matmul_mx(
+                out=q_banks[t][:],
+                lhsT=db[:, t * P : (t + 1) * P].bitcast(FP8X4),
+                lhsT_scale=ds[4:P, t * P : (t + 1) * P],
+                rhs=codes[1][:].bitcast(FP8X4),
+                rhs_scale=scales[1][:],
+                start=True,
+                stop=True,
+            )
+        for t in range(PACK):
+            if t + 1 < PACK:
+                nc.scalar.copy(p_src[t + 1], p_banks[t + 1][:])
+            nc.scalar.copy(q_src[t], q_banks[t][:])
+
+        y = tile("y", PACK * J, F32)
+        y_rounded = tile("y_rounded", PACK * J, BF16)
+        y_codes = tile("y_codes", J, U32)
+        y_scales = tile("y_scales", J, U8)
+        out_rows = out_0.rearrange("(p t) j -> p t j", t=PACK)
+        out_words = out_1[0].rearrange("p c r -> p (c r)").bitcast(I32)
+
+        def round_pair(copy, t, cols):
+            copy(
+                y_rounded[:].rearrange("p (j t) -> p j t", t=PACK)[:, cols, t : t + 2],
+                y[:].rearrange("p (t j) -> p j t", t=PACK)[:, cols, t : t + 2],
+            )
+
+        def add_pages(t, cols):
+            dst = y[:, t * J + cols.start : t * J + cols.stop]
+            nc.vector.tensor_tensor(dst, p_pages[t % 2][:, cols], q_page[:, cols], ADD)
+            nc.sync.dma_start(out_rows[:, t, cols], dst)
+
+        for t in range(PACK):
+            if t + 1 < PACK:
+                nc.vector.tensor_copy(p_pages[(t + 1) % 2][:].indirect(list2[:]), p_src[t + 1])
+            nc.vector.tensor_copy(q_page[:].indirect(list3[:]), q_src[t])
+            if t + 1 < PACK:
+                add_pages(t, slice(0, J))
+            if t == 1:
+                round_pair(nc.scalar.copy, 0, slice(0, J))
+
+        first, second = slice(0, BANK), slice(BANK, J)
+        add_pages(PACK - 1, first)
+        add_pages(PACK - 1, second)
+        round_pair(nc.scalar.copy, 2, first)
+        round_pair(nc.vector.tensor_copy, 2, second)
+        for cols in (second, first):
+            nc.vector.quantize_mx(
+                out=y_codes[:, cols].bitcast(FP8X4),
+                scales=y_scales[:, cols],
+                in_=y_rounded[:, PACK * cols.start : PACK * cols.stop],
+            )
+            nc.sync.dma_start(out_words[:, cols], y_codes[:, cols].bitcast(I32))
+        for q in range(4):
+            nc.scalar.dma_start(
+                out_2[0, 4 * q : 4 * q + 4, :].bitcast(I32), y_scales[32 * q : 32 * q + 4, :].bitcast(I32)
+            )

@@ -43,54 +43,59 @@ def tile_list_expert_down_two_roads_pl_kernel(
         list2 = lists.tile([P, I // 16], U16, name="list2")
         list3 = lists.tile([P, S // 16], U16, name="list3")
 
-        xs_rows = sb.tile([P, T], U8, name="xs_rows", tag="xs_rows", align_bytes=64)
+        xs_rows = tile("xs_rows", T, U8)
         xs_picked = tile("xs_picked", J, U8)
-        xs = tile("xs", PASSES * J, U8)
+        xs_moved = tile("xs_moved", J, U8)
         xw = [tile("xw%d" % z, T, U16) for z in range(PASSES)]
         wa_raw = tile("wa_raw", PASSES * R, I32)
         was_raw = tile("was_raw", PASSES * R, U8)
-        da_raw = tile("da_raw", 2 * N, U8)
-        db_raw = tile("db_raw", N, I32)
         p_pages = [tile("p_page%d" % u, J, F32) for u in range(2)]
-        q_page = tile("q_page", J, F32)
+        q_pages = [tile("q_page%d" % u, J, F32) for u in range(2)]
+        queues = [nc.sync, nc.sync, nc.scalar, nc.scalar]
 
         nc.sync.dma_start(list1[:], offs)
-        nc.sync.dma_start(
-            xs_rows[0:32, :].bitcast(I32), xq_scales.rearrange("z q c -> (z q) c").bitcast(I32)
-        )
-        for z in range(PASSES):
-            nc.sync.dma_start(xw[z][:].bitcast(I32), xq_words[z].bitcast(I32))
+        for plane in (xs_rows, was_raw, xs_moved):
+            nc.gpsimd.memset(plane[:].bitcast(I32), 0)
+        for q in range(4):
+            queues[q].dma_start(
+                xs_rows[32 * q : 32 * q + 8, :].bitcast(I32), xq_scales[:, 4 * q : 4 * q + 4, :].bitcast(I32)
+            )
         nc.sync.dma_start(
             wa_raw[:].rearrange("p (z c) -> p z c", z=PASSES),
             wa_words.rearrange("z p c r -> p z (c r)").bitcast(I32),
         )
-        nc.vector.memset(xs_rows[32:64, :].bitcast(I32), 0)
-        nc.vector.memset(xs_rows[64:128, :].bitcast(I32), 0)
-        nc.vector.memset(was_raw[:].bitcast(I32), 0)
-        nc.vector.memset(xs[:].bitcast(I32), 0)
         for q in range(4):
-            nc.sync.dma_start(
+            queues[q].dma_start(
                 was_raw[32 * q : 32 * q + 4, :].bitcast(I32).rearrange("r (z c) -> r z c", z=PASSES),
                 wa_scales[:, 4 * q : 4 * q + 4, :].bitcast(I32).rearrange("z r c -> r z c"),
             )
+        nc.scalar.dma_start(xw[0][:].bitcast(I32), xq_words[0].bitcast(I32))
+        nc.sync.dma_start(xw[1][:].bitcast(I32), xq_words[1].bitcast(I32))
         nc.sync.dma_start(list2[:], offs2)
         nc.sync.dma_start(list3[:], offs3)
-        nc.sync.dma_start(da_raw[:].bitcast(I32), da_words[0].bitcast(I32))
-        nc.sync.dma_start(db_raw[:], db_words[0].rearrange("p c r -> p (c r)").bitcast(I32))
-        for page in p_pages + [q_page]:
-            nc.vector.memset(page[:], 0.0)
+        for page in p_pages + q_pages:
+            nc.gpsimd.memset(page[:], 0.0)
 
         nc.vector.tensor_copy(xs_picked[:], xs_rows[:].indirect(list1[:]))
-        for z in range(PASSES):
-            for q in range(4):
-                row = 16 * z + 4 * q
-                (nc.scalar if q % 2 else nc.sync).dma_start(
-                    xs[32 * q : 32 * q + 4, z * J : (z + 1) * J].bitcast(I32),
-                    xs_picked[row : row + 4, :].bitcast(I32),
-                )
+        nc.scalar.dma_start(xs_moved[0:100, :].bitcast(I32), xs_picked[4:104, :].bitcast(I32))
+        xs = [xs_picked, xs_moved]
 
-        ds_raw = sb.tile([P, N], U8, name="ds_raw", tag="xs_rows", align_bytes=64)
-        nc.vector.memset(ds_raw[:].bitcast(I32), 0)
+        wa = tile("wa", PASSES * R, I32)
+        was = tile("was", PASSES * R, U8)
+        nc.vector.tensor_copy(
+            wa[:].rearrange("p (z t c i) -> p z c t i", z=PASSES, t=PACK, i=4),
+            wa_raw[:].rearrange("p (z c i t) -> p z c t i", z=PASSES, t=PACK, i=4),
+        )
+        nc.gpsimd.tensor_copy(
+            was[:].rearrange("p (z t m) -> p z t m", z=PASSES, t=PACK),
+            was_raw[:].rearrange("p (z m t) -> p z t m", z=PASSES, t=PACK),
+        )
+        db_raw = tile("xs_rows", N, I32)
+        da_raw = tile("was_raw", 2 * N, U8)
+        nc.sync.dma_start(db_raw[:], db_words[0].rearrange("p c r -> p (c r)").bitcast(I32))
+        nc.sync.dma_start(da_raw[:].bitcast(I32), da_words[0].bitcast(I32))
+        ds_raw = tile("wa_raw", N, U8)
+        nc.gpsimd.memset(ds_raw[:].bitcast(I32), 0)
         for q in range(4):
             nc.sync.dma_start(
                 ds_raw[32 * q : 32 * q + 4, :].bitcast(I32), da_scales[0, 4 * q : 4 * q + 4, :].bitcast(I32)
@@ -99,60 +104,51 @@ def tile_list_expert_down_two_roads_pl_kernel(
                 ds_raw[32 * q + 4 : 32 * q + 8, :].bitcast(I32), db_scales[0, 4 * q : 4 * q + 4, :].bitcast(I32)
             )
 
-        wa = tile("wa", PASSES * R, I32)
-        was = tile("was", PASSES * R, U8)
         hid = tile("hid", PACK * J, F32)
         xg = {}
-
-        def pick_words(h):
-            for z in range(PASSES):
+        for z in range(PASSES):
+            for h in range(HALVES):
                 xg[(z, h)] = tile("xg%d%d" % (z, h), BANK, U16)
                 cols = slice(h * BANK // 16, (h + 1) * BANK // 16)
                 nc.vector.tensor_copy(xg[(z, h)][:], xw[z][:].indirect(list1[:, cols]))
 
-        def hidden(h):
-            banks = [bank(PACK * h + t) for t in range(PACK)]
-            for z in range(PASSES):
-                for t in range(PACK):
-                    cols = slice(z * R + t * P, z * R + (t + 1) * P)
-                    nc.tensor.matmul_mx(
-                        out=banks[t][:],
-                        lhsT=wa[:, cols].bitcast(FP8X4),
-                        lhsT_scale=was[:, cols],
-                        rhs=xg[(z, h)][:].bitcast(FP4X4),
-                        rhs_scale=xs[:, z * J + h * BANK : z * J + (h + 1) * BANK],
-                        start=(z == 0),
-                        stop=(z == PASSES - 1),
-                    )
-            for t in range(PACK):
-                nc.scalar.activation(hid[:, t * J + h * BANK : t * J + (h + 1) * BANK], banks[t][:], RELU)
+        hid_banks = {(t, h): bank(HALVES * t + h) for t in range(PACK) for h in range(HALVES)}
 
-        pick_words(0)
-        nc.vector.tensor_copy(
-            wa[:].rearrange("p (z t c i) -> p z c t i", z=PASSES, t=PACK, i=4),
-            wa_raw[:].rearrange("p (z c i t) -> p z c t i", z=PASSES, t=PACK, i=4),
-        )
-        nc.vector.tensor_copy(
-            was[:].rearrange("p (z t m) -> p z t m", z=PASSES, t=PACK),
-            was_raw[:].rearrange("p (z m t) -> p z t m", z=PASSES, t=PACK),
-        )
-        hidden(0)
-        pick_words(1)
-        hidden(1)
+        def hidden_pass(z, t, h):
+            cols = slice(z * R + t * P, z * R + (t + 1) * P)
+            nc.tensor.matmul_mx(
+                out=hid_banks[(t, h)][:],
+                lhsT=wa[:, cols].bitcast(FP8X4),
+                lhsT_scale=was[:, cols],
+                rhs=xg[(z, h)][:].bitcast(FP4X4),
+                rhs_scale=xs[z][:, h * BANK : (h + 1) * BANK],
+                start=(z == 0),
+                stop=(z == PASSES - 1),
+            )
+
+        for h in range(HALVES):
+            for t in range(PACK):
+                hidden_pass(0, t, h)
+        for t in range(PACK):
+            for h in range(HALVES):
+                hidden_pass(1, t, h)
+                nc.scalar.activation(
+                    hid[:, t * J + h * BANK : t * J + (h + 1) * BANK], hid_banks[(t, h)][:], RELU
+                )
 
         da = tile("da", 2 * N, U8)
         db = tile("db", N, I32)
         ds = tile("ds", N, U8)
-        nc.vector.tensor_copy(
+        nc.gpsimd.tensor_copy(
             da[:].rearrange("p (t m b) -> p t m b", t=PACK, b=2),
             da_raw[:].rearrange("p (m t b) -> p t m b", t=PACK, b=2),
         )
-        nc.vector.tensor_copy(
-            ds[:].rearrange("p (t m) -> p t m", t=PACK), ds_raw[:].rearrange("p (m t) -> p t m", t=PACK)
-        )
-        nc.vector.tensor_copy(
+        nc.gpsimd.tensor_copy(
             db[:].rearrange("p (t c i) -> p c t i", t=PACK, i=4),
             db_raw[:].rearrange("p (c i t) -> p c t i", t=PACK, i=4),
+        )
+        nc.gpsimd.tensor_copy(
+            ds[:].rearrange("p (t m) -> p t m", t=PACK), ds_raw[:].rearrange("p (m t) -> p t m", t=PACK)
         )
 
         picked_a = tile("picked_a", PACK * I, F32)
@@ -226,23 +222,23 @@ def tile_list_expert_down_two_roads_pl_kernel(
                 y[:].rearrange("p (t j) -> p j t", t=PACK)[:, cols, t : t + 2],
             )
 
-        def add_pages(t, cols):
+        def add_pages(engine, t, cols):
             dst = y[:, t * J + cols.start : t * J + cols.stop]
-            nc.vector.tensor_tensor(dst, p_pages[t % 2][:, cols], q_page[:, cols], ADD)
+            engine.tensor_tensor(dst, p_pages[t % 2][:, cols], q_pages[t % 2][:, cols], ADD)
             nc.sync.dma_start(out_rows[:, t, cols], dst)
 
         for t in range(PACK):
             if t + 1 < PACK:
                 nc.vector.tensor_copy(p_pages[(t + 1) % 2][:].indirect(list2[:]), p_src[t + 1])
-            nc.vector.tensor_copy(q_page[:].indirect(list3[:]), q_src[t])
+            nc.vector.tensor_copy(q_pages[t % 2][:].indirect(list3[:]), q_src[t])
             if t + 1 < PACK:
-                add_pages(t, slice(0, J))
+                add_pages(nc.gpsimd, t, slice(0, J))
             if t == 1:
                 round_pair(nc.scalar.copy, 0, slice(0, J))
 
         first, second = slice(0, BANK), slice(BANK, J)
-        add_pages(PACK - 1, first)
-        add_pages(PACK - 1, second)
+        add_pages(nc.vector, PACK - 1, first)
+        add_pages(nc.vector, PACK - 1, second)
         round_pair(nc.scalar.copy, 2, first)
         round_pair(nc.vector.tensor_copy, 2, second)
         for cols in (second, first):

@@ -75,6 +75,15 @@ def tile_list_expert_down_two_roads_pl_kernel(
         nc.sync.dma_start(list3[:], offs3)
         for page in p_pages + q_pages:
             nc.gpsimd.memset(page[:], 0.0)
+        ds_raw = tile("ds_raw", N, U8)
+        nc.gpsimd.memset(ds_raw[:].bitcast(I32), 0)
+        for q in range(4):
+            nc.sync.dma_start(
+                ds_raw[32 * q : 32 * q + 4, :].bitcast(I32), da_scales[0, 4 * q : 4 * q + 4, :].bitcast(I32)
+            )
+            nc.sync.dma_start(
+                ds_raw[32 * q + 4 : 32 * q + 8, :].bitcast(I32), db_scales[0, 4 * q : 4 * q + 4, :].bitcast(I32)
+            )
 
         nc.vector.tensor_copy(xs_picked[:], xs_rows[:].indirect(list1[:]))
         nc.scalar.dma_start(xs_moved[0:100, :].bitcast(I32), xs_picked[4:104, :].bitcast(I32))
@@ -86,29 +95,20 @@ def tile_list_expert_down_two_roads_pl_kernel(
             wa[:].rearrange("p (z t c i) -> p z c t i", z=PASSES, t=PACK, i=4),
             wa_raw[:].rearrange("p (z c i t) -> p z c t i", z=PASSES, t=PACK, i=4),
         )
-        nc.gpsimd.tensor_copy(
+        nc.vector.tensor_copy(
             was[:].rearrange("p (z t m) -> p z t m", z=PASSES, t=PACK),
             was_raw[:].rearrange("p (z m t) -> p z t m", z=PASSES, t=PACK),
         )
         db_raw = tile("xs_rows", N, I32)
-        da_raw = tile("was_raw", 2 * N, U8)
         nc.sync.dma_start(db_raw[:], db_words[0].rearrange("p c r -> p (c r)").bitcast(I32))
-        nc.sync.dma_start(da_raw[:].bitcast(I32), da_words[0].bitcast(I32))
-        ds_raw = tile("wa_raw", N, U8)
-        nc.gpsimd.memset(ds_raw[:].bitcast(I32), 0)
-        for q in range(4):
-            nc.sync.dma_start(
-                ds_raw[32 * q : 32 * q + 4, :].bitcast(I32), da_scales[0, 4 * q : 4 * q + 4, :].bitcast(I32)
-            )
-            nc.sync.dma_start(
-                ds_raw[32 * q + 4 : 32 * q + 8, :].bitcast(I32), db_scales[0, 4 * q : 4 * q + 4, :].bitcast(I32)
-            )
+        da_raw = tile("wa_raw", 2 * N, U8)
+        nc.scalar.dma_start(da_raw[:].bitcast(I32), da_words[0].bitcast(I32))
 
         hid = tile("hid", PACK * J, F32)
         xg = {}
         for z in range(PASSES):
             for h in range(HALVES):
-                xg[(z, h)] = tile("xg%d%d" % (z, h), BANK, U16)
+                xg[(z, h)] = tile("was_raw" if (z, h) == (0, 1) else "xg%d%d" % (z, h), BANK, U16)
                 cols = slice(h * BANK // 16, (h + 1) * BANK // 16)
                 nc.vector.tensor_copy(xg[(z, h)][:], xw[z][:].indirect(list1[:, cols]))
 
@@ -139,15 +139,15 @@ def tile_list_expert_down_two_roads_pl_kernel(
         da = tile("da", 2 * N, U8)
         db = tile("db", N, I32)
         ds = tile("ds", N, U8)
-        nc.gpsimd.tensor_copy(
+        nc.vector.tensor_copy(
             da[:].rearrange("p (t m b) -> p t m b", t=PACK, b=2),
             da_raw[:].rearrange("p (m t b) -> p t m b", t=PACK, b=2),
         )
-        nc.gpsimd.tensor_copy(
+        nc.vector.tensor_copy(
             db[:].rearrange("p (t c i) -> p c t i", t=PACK, i=4),
             db_raw[:].rearrange("p (c i t) -> p c t i", t=PACK, i=4),
         )
-        nc.gpsimd.tensor_copy(
+        nc.vector.tensor_copy(
             ds[:].rearrange("p (t m) -> p t m", t=PACK), ds_raw[:].rearrange("p (m t) -> p t m", t=PACK)
         )
 

@@ -1,6 +1,7 @@
 from contextlib import ExitStack
 
 import concourse.mybir as mybir
+from concourse.masks import make_identity
 
 K, T, J, I, S, R, N = 1024, 2048, 1024, 512, 512, 512, 512
 FLOPS = 2 * K * R * J + 2 * R * N * I + 2 * R * N * S
@@ -49,8 +50,6 @@ def tile_list_expert_down_two_roads_pl_kernel(
         xw = [tile("xw%d" % z, T, U16) for z in range(PASSES)]
         wa_raw = tile("wa_raw", PASSES * R, I32)
         was_raw = tile("was_raw", PASSES * R, U8)
-        p_pages = [tile("p_page%d" % u, J, F32) for u in range(2)]
-        q_pages = [tile("q_page%d" % u, J, F32) for u in range(2)]
         queues = [nc.sync, nc.sync, nc.scalar, nc.scalar]
 
         nc.sync.dma_start(list1[:], offs)
@@ -73,8 +72,6 @@ def tile_list_expert_down_two_roads_pl_kernel(
         nc.sync.dma_start(xw[1][:].bitcast(I32), xq_words[1].bitcast(I32))
         nc.sync.dma_start(list2[:], offs2)
         nc.sync.dma_start(list3[:], offs3)
-        for page in p_pages + q_pages:
-            nc.gpsimd.memset(page[:], 0.0)
         ds_raw = tile("ds_raw", N, U8)
         nc.gpsimd.memset(ds_raw[:].bitcast(I32), 0)
         for q in range(4):
@@ -84,9 +81,13 @@ def tile_list_expert_down_two_roads_pl_kernel(
             nc.sync.dma_start(
                 ds_raw[32 * q + 4 : 32 * q + 8, :].bitcast(I32), db_scales[0, 4 * q : 4 * q + 4, :].bitcast(I32)
             )
+        ident = tile("ident", P, F32)
+        make_identity(nc, ident[:])
 
-        nc.vector.tensor_copy(xs_picked[:], xs_rows[:].indirect(list1[:]))
-        nc.scalar.dma_start(xs_moved[0:100, :].bitcast(I32), xs_picked[4:104, :].bitcast(I32))
+        for h in range(HALVES):
+            cols = slice(h * BANK, (h + 1) * BANK)
+            nc.vector.tensor_copy(xs_picked[:, cols], xs_rows[:].indirect(list1[:, h * BANK // 16 : (h + 1) * BANK // 16]))
+            nc.scalar.dma_start(xs_moved[0:100, cols].bitcast(I32), xs_picked[4:104, cols].bitcast(I32))
         xs = [xs_picked, xs_moved]
 
         wa = tile("wa", PASSES * R, I32)
@@ -95,7 +96,7 @@ def tile_list_expert_down_two_roads_pl_kernel(
             wa[:].rearrange("p (z t c i) -> p z c t i", z=PASSES, t=PACK, i=4),
             wa_raw[:].rearrange("p (z c i t) -> p z c t i", z=PASSES, t=PACK, i=4),
         )
-        nc.vector.tensor_copy(
+        nc.gpsimd.tensor_copy(
             was[:].rearrange("p (z t m) -> p z t m", z=PASSES, t=PACK),
             was_raw[:].rearrange("p (z m t) -> p z t m", z=PASSES, t=PACK),
         )
@@ -126,30 +127,40 @@ def tile_list_expert_down_two_roads_pl_kernel(
                 stop=(z == PASSES - 1),
             )
 
-        for h in range(HALVES):
+        def relu_out(t, h):
+            nc.scalar.activation(hid[:, t * J + h * BANK : t * J + (h + 1) * BANK], hid_banks[(t, h)][:], RELU)
+
+        for z in range(PASSES):
             for t in range(PACK):
-                hidden_pass(0, t, h)
+                hidden_pass(z, t, 0)
         for t in range(PACK):
-            for h in range(HALVES):
-                hidden_pass(1, t, h)
-                nc.scalar.activation(
-                    hid[:, t * J + h * BANK : t * J + (h + 1) * BANK], hid_banks[(t, h)][:], RELU
-                )
+            relu_out(t, 0)
+        for t in range(PACK):
+            for z in range(PASSES):
+                hidden_pass(z, t, 1)
+            if t == 0:
+                nc.vector.tensor_scalar_max(hid[:, BANK:J], hid_banks[(0, 1)][:], 0.0)
+            else:
+                relu_out(t, 1)
 
         da = tile("da", 2 * N, U8)
         db = tile("db", N, I32)
         ds = tile("ds", N, U8)
-        nc.vector.tensor_copy(
+        nc.gpsimd.tensor_copy(
             da[:].rearrange("p (t m b) -> p t m b", t=PACK, b=2),
             da_raw[:].rearrange("p (m t b) -> p t m b", t=PACK, b=2),
         )
-        nc.vector.tensor_copy(
+        nc.gpsimd.tensor_copy(
             db[:].rearrange("p (t c i) -> p c t i", t=PACK, i=4),
             db_raw[:].rearrange("p (c i t) -> p c t i", t=PACK, i=4),
         )
-        nc.vector.tensor_copy(
+        nc.gpsimd.tensor_copy(
             ds[:].rearrange("p (t m) -> p t m", t=PACK), ds_raw[:].rearrange("p (m t) -> p t m", t=PACK)
         )
+        p_pages = [tile(slot, J, F32) for slot in ("xw0", "xw1")]
+        q_pages = [tile(slot, J, F32) for slot in ("xs_rows", "wa_raw")]
+        for page in p_pages + q_pages:
+            nc.gpsimd.memset(page[:], 0.0)
 
         picked_a = tile("picked_a", PACK * I, F32)
         work = tile("work", PACK * S, F32)
@@ -178,6 +189,7 @@ def tile_list_expert_down_two_roads_pl_kernel(
 
         p_src = [staged[:, 0:BANK]] + [work[:, u * BANK : (u + 1) * BANK] for u in range(3)]
         q_src = [staged[:, (u + 1) * BANK : (u + 2) * BANK] for u in range(PACK)]
+        p_src[2] = q_src[0]
         p_banks = [bank(t) for t in range(PACK)]
         for t in range(PACK):
             nc.tensor.matmul_mx(
@@ -189,6 +201,8 @@ def tile_list_expert_down_two_roads_pl_kernel(
                 start=True,
                 stop=True,
             )
+        p_pages.append(tile("codes0", J, F32))
+        nc.gpsimd.memset(p_pages[2][:], 0.0)
         nc.scalar.copy(p_src[0], p_banks[0][:])
         interleave(rounded_b[:], work[:])
         nc.vector.tensor_copy(p_pages[0][:].indirect(list2[:]), p_src[0])
@@ -204,8 +218,10 @@ def tile_list_expert_down_two_roads_pl_kernel(
                 start=True,
                 stop=True,
             )
+        q_pages.append(tile("codes1", J, F32))
+        nc.gpsimd.memset(q_pages[2][:], 0.0)
         for t in range(PACK):
-            if t + 1 < PACK:
+            if t in (0, 2):
                 nc.scalar.copy(p_src[t + 1], p_banks[t + 1][:])
             nc.scalar.copy(q_src[t], q_banks[t][:])
 
@@ -224,15 +240,38 @@ def tile_list_expert_down_two_roads_pl_kernel(
 
         def add_pages(engine, t, cols):
             dst = y[:, t * J + cols.start : t * J + cols.stop]
-            engine.tensor_tensor(dst, p_pages[t % 2][:, cols], q_pages[t % 2][:, cols], ADD)
+            engine.tensor_tensor(dst, p_pages[t % 3][:, cols], q_pages[t % 3][:, cols], ADD)
             nc.sync.dma_start(out_rows[:, t, cols], dst)
 
+        def add_pages_turned(t):
+            blocks = [slice(b * P, (b + 1) * P) for b in range(BANK // P)]
+            turned = []
+            for h in range(HALVES):
+                summed = bank((0, 4, 6)[t] + h)
+                for blk in blocks:
+                    cols = slice(h * BANK + blk.start, h * BANK + blk.stop)
+                    for first, page in ((True, p_pages[t % 3]), (False, q_pages[t % 3])):
+                        nc.tensor.matmul(
+                            summed[:, blk], page[:, cols], ident[:], start=first, stop=not first, is_transpose=True
+                        )
+                turned.append(y[:, 3 * J + h * BANK : 3 * J + (h + 1) * BANK])
+                nc.scalar.copy(turned[h], summed[:])
+            for h in range(HALVES):
+                back = bank((2, 6, 0)[t] + h)
+                for blk in blocks:
+                    nc.tensor.transpose(back[:, blk], turned[h][:, blk], ident[:])
+                nc.scalar.copy(y[:, t * J + h * BANK : t * J + (h + 1) * BANK], back[:])
+            nc.scalar.dma_start(out_rows[:, t, :], y[:, t * J : (t + 1) * J])
+
+        nc.vector.tensor_copy(p_pages[1][:].indirect(list2[:]), p_src[1])
         for t in range(PACK):
-            if t + 1 < PACK:
-                nc.vector.tensor_copy(p_pages[(t + 1) % 2][:].indirect(list2[:]), p_src[t + 1])
-            nc.vector.tensor_copy(q_pages[t % 2][:].indirect(list3[:]), q_src[t])
-            if t + 1 < PACK:
-                add_pages(nc.gpsimd, t, slice(0, J))
+            if t >= 2:
+                nc.vector.tensor_copy(p_pages[t % 3][:].indirect(list2[:]), p_src[t])
+            nc.vector.tensor_copy(q_pages[t % 3][:].indirect(list3[:]), q_src[t])
+            if t == 0:
+                nc.scalar.copy(p_src[2], p_banks[2][:])
+            if t < 3:
+                add_pages_turned(t)
             if t == 1:
                 round_pair(nc.scalar.copy, 0, slice(0, J))
 

from contextlib import ExitStack

import concourse.mybir as mybir
from concourse.masks import make_identity

K, T, J, I, S, R, N = 1024, 2048, 1024, 512, 512, 512, 512
FLOPS = 2 * K * R * J + 2 * R * N * I + 2 * R * N * S

F32 = mybir.dt.float32
BF16 = mybir.dt.bfloat16
I32 = mybir.dt.int32
U32 = mybir.dt.uint32
U16 = mybir.dt.uint16
U8 = mybir.dt.uint8
FP8X4 = mybir.dt.float8_e4m3fn_x4
FP4X4 = mybir.dt.float4_e2m1fn_x4
RELU = mybir.ActivationFunctionType.Relu
ADD = mybir.AluOpType.add

P = 128
PACK = 4
BANK = 512
PASSES = K // (P * PACK)
HALVES = J // BANK


def tile_list_expert_down_two_roads_pl_kernel(
    tc, xq_words, xq_scales, wa_words, wa_scales, da_words, da_scales, db_words, db_scales,
    offs, offs2, offs3, out_0, out_1, out_2,
):
    nc = tc.nc
    with ExitStack() as ctx:
        lists = ctx.enter_context(tc.tile_pool(name="lists", bufs=1))
        sb = ctx.enter_context(tc.tile_pool(name="sb", bufs=1))
        psum = ctx.enter_context(tc.psum_pool(name="psum", bufs=1))

        def tile(name, cols, dtype):
            return sb.tile([P, cols], dtype, name=name, align_bytes=64)

        def bank(b):
            return psum.tile([P, BANK], F32, name="bank%d" % b)

        list1 = lists.tile([P, J // 16], U16, name="list1")
        list2 = lists.tile([P, I // 16], U16, name="list2")
        list3 = lists.tile([P, S // 16], U16, name="list3")

        xs_rows = tile("xs_rows", T, U8)
        xs_picked = tile("xs_picked", J, U8)
        xs_moved = tile("xs_moved", J, U8)
        xw = [tile("xw%d" % z, T, U16) for z in range(PASSES)]
        wa_raw = tile("wa_raw", PASSES * R, I32)
        was_raw = tile("was_raw", PASSES * R, U8)
        queues = [nc.sync, nc.sync, nc.scalar, nc.scalar]

        nc.sync.dma_start(list1[:], offs)
        for plane in (xs_rows, was_raw, xs_moved):
            nc.gpsimd.memset(plane[:].bitcast(I32), 0)
        for q in range(4):
            queues[q].dma_start(
                xs_rows[32 * q : 32 * q + 8, :].bitcast(I32), xq_scales[:, 4 * q : 4 * q + 4, :].bitcast(I32)
            )
        nc.sync.dma_start(
            wa_raw[:].rearrange("p (z c) -> p z c", z=PASSES),
            wa_words.rearrange("z p c r -> p z (c r)").bitcast(I32),
        )
        for q in range(4):
            queues[q].dma_start(
                was_raw[32 * q : 32 * q + 4, :].bitcast(I32).rearrange("r (z c) -> r z c", z=PASSES),
                wa_scales[:, 4 * q : 4 * q + 4, :].bitcast(I32).rearrange("z r c -> r z c"),
            )
        nc.scalar.dma_start(xw[0][:].bitcast(I32), xq_words[0].bitcast(I32))
        nc.sync.dma_start(xw[1][:].bitcast(I32), xq_words[1].bitcast(I32))
        nc.sync.dma_start(list2[:], offs2)
        nc.sync.dma_start(list3[:], offs3)
        ds_raw = tile("ds_raw", N, U8)
        nc.gpsimd.memset(ds_raw[:].bitcast(I32), 0)
        for q in range(4):
            nc.sync.dma_start(
                ds_raw[32 * q : 32 * q + 4, :].bitcast(I32), da_scales[0, 4 * q : 4 * q + 4, :].bitcast(I32)
            )
            nc.sync.dma_start(
                ds_raw[32 * q + 4 : 32 * q + 8, :].bitcast(I32), db_scales[0, 4 * q : 4 * q + 4, :].bitcast(I32)
            )
        ident = tile("ident", P, F32)
        make_identity(nc, ident[:])

        for h in range(HALVES):
            cols = slice(h * BANK, (h + 1) * BANK)
            nc.vector.tensor_copy(xs_picked[:, cols], xs_rows[:].indirect(list1[:, h * BANK // 16 : (h + 1) * BANK // 16]))
            nc.scalar.dma_start(xs_moved[0:100, cols].bitcast(I32), xs_picked[4:104, cols].bitcast(I32))
        xs = [xs_picked, xs_moved]

        wa = tile("wa", PASSES * R, I32)
        was = tile("was", PASSES * R, U8)
        nc.vector.tensor_copy(
            wa[:].rearrange("p (z t c i) -> p z c t i", z=PASSES, t=PACK, i=4),
            wa_raw[:].rearrange("p (z c i t) -> p z c t i", z=PASSES, t=PACK, i=4),
        )
        nc.gpsimd.tensor_copy(
            was[:].rearrange("p (z t m) -> p z t m", z=PASSES, t=PACK),
            was_raw[:].rearrange("p (z m t) -> p z t m", z=PASSES, t=PACK),
        )
        db_raw = tile("xs_rows", N, I32)
        nc.sync.dma_start(db_raw[:], db_words[0].rearrange("p c r -> p (c r)").bitcast(I32))
        da_raw = tile("wa_raw", 2 * N, U8)
        nc.scalar.dma_start(da_raw[:].bitcast(I32), da_words[0].bitcast(I32))

        hid = tile("hid", PACK * J, F32)
        xg = {}
        for z in range(PASSES):
            for h in range(HALVES):
                xg[(z, h)] = tile("was_raw" if (z, h) == (0, 1) else "xg%d%d" % (z, h), BANK, U16)
                cols = slice(h * BANK // 16, (h + 1) * BANK // 16)
                nc.vector.tensor_copy(xg[(z, h)][:], xw[z][:].indirect(list1[:, cols]))

        hid_banks = {(t, h): bank(HALVES * t + h) for t in range(PACK) for h in range(HALVES)}

        def hidden_pass(z, t, h):
            cols = slice(z * R + t * P, z * R + (t + 1) * P)
            nc.tensor.matmul_mx(
                out=hid_banks[(t, h)][:],
                lhsT=wa[:, cols].bitcast(FP8X4),
                lhsT_scale=was[:, cols],
                rhs=xg[(z, h)][:].bitcast(FP4X4),
                rhs_scale=xs[z][:, h * BANK : (h + 1) * BANK],
                start=(z == 0),
                stop=(z == PASSES - 1),
            )

        def relu_out(t, h):
            nc.scalar.activation(hid[:, t * J + h * BANK : t * J + (h + 1) * BANK], hid_banks[(t, h)][:], RELU)

        for z in range(PASSES):
            for t in range(PACK):
                hidden_pass(z, t, 0)
        for t in range(PACK):
            relu_out(t, 0)
        for t in range(PACK):
            for z in range(PASSES):
                hidden_pass(z, t, 1)
            if t == 0:
                nc.vector.tensor_scalar_max(hid[:, BANK:J], hid_banks[(0, 1)][:], 0.0)
            else:
                relu_out(t, 1)

        da = tile("da", 2 * N, U8)
        db = tile("db", N, I32)
        ds = tile("ds", N, U8)
        nc.gpsimd.tensor_copy(
            da[:].rearrange("p (t m b) -> p t m b", t=PACK, b=2),
            da_raw[:].rearrange("p (m t b) -> p t m b", t=PACK, b=2),
        )
        nc.gpsimd.tensor_copy(
            db[:].rearrange("p (t c i) -> p c t i", t=PACK, i=4),
            db_raw[:].rearrange("p (c i t) -> p c t i", t=PACK, i=4),
        )
        nc.gpsimd.tensor_copy(
            ds[:].rearrange("p (t m) -> p t m", t=PACK), ds_raw[:].rearrange("p (m t) -> p t m", t=PACK)
        )
        p_pages = [tile(slot, J, F32) for slot in ("xw0", "xw1")]
        q_pages = [tile(slot, J, F32) for slot in ("xs_rows", "wa_raw")]
        for page in p_pages + q_pages:
            nc.gpsimd.memset(page[:], 0.0)

        picked_a = tile("picked_a", PACK * I, F32)
        work = tile("work", PACK * S, F32)
        rounded_a = work[:, 2 * S : 4 * S].bitcast(BF16)
        rounded_b = tile("rounded_b", PACK * S, BF16)
        codes = [tile("codes%d" % u, BANK, U32) for u in range(2)]
        scales = [tile("scales%d" % u, BANK, U8) for u in range(2)]
        staged = tile("staged", 5 * BANK, F32)

        def interleave(dst, src):
            nc.scalar.copy(
                dst.rearrange("p (c i t) -> p c t i", t=PACK, i=4),
                src.rearrange("p (t c i) -> p c t i", t=PACK, i=4),
            )

        for t in range(PACK):
            nc.vector.tensor_copy(
                picked_a[:, t * I : (t + 1) * I], hid[:, t * J : (t + 1) * J].indirect(list2[:])
            )
        interleave(rounded_a, picked_a[:])
        for t in range(2):
            nc.vector.tensor_copy(work[:, t * S : (t + 1) * S], hid[:, t * J :].indirect(list3[:]))
        nc.vector.quantize_mx(out=codes[0][:].bitcast(FP8X4), scales=scales[0][:], in_=rounded_a)
        for t in range(2, PACK):
            nc.vector.tensor_copy(work[:, t * S : (t + 1) * S], hid[:, t * J :].indirect(list3[:]))

        p_src = [staged[:, 0:BANK]] + [work[:, u * BANK : (u + 1) * BANK] for u in range(3)]
        q_src = [staged[:, (u + 1) * BANK : (u + 2) * BANK] for u in range(PACK)]
        p_src[2] = q_src[0]
        p_banks = [bank(t) for t in range(PACK)]
        for t in range(PACK):
            nc.tensor.matmul_mx(
                out=p_banks[t][:],
                lhsT=da[:, 2 * t * P : 2 * (t + 1) * P].bitcast(FP4X4),
                lhsT_scale=ds[:, t * P : (t + 1) * P],
                rhs=codes[0][:].bitcast(FP8X4),
                rhs_scale=scales[0][:],
                start=True,
                stop=True,
            )
        p_pages.append(tile("codes0", J, F32))
        nc.gpsimd.memset(p_pages[2][:], 0.0)
        nc.scalar.copy(p_src[0], p_banks[0][:])
        interleave(rounded_b[:], work[:])
        nc.vector.tensor_copy(p_pages[0][:].indirect(list2[:]), p_src[0])
        nc.vector.quantize_mx(out=codes[1][:].bitcast(FP8X4), scales=scales[1][:], in_=rounded_b[:])
        q_banks = [bank(PACK + t) for t in range(PACK)]
        for t in range(PACK):
            nc.tensor.matmul_mx(
                out=q_banks[t][:],
                lhsT=db[:, t * P : (t + 1) * P].bitcast(FP8X4),
                lhsT_scale=ds[4:P, t * P : (t + 1) * P],
                rhs=codes[1][:].bitcast(FP8X4),
                rhs_scale=scales[1][:],
                start=True,
                stop=True,
            )
        q_pages.append(tile("codes1", J, F32))
        nc.gpsimd.memset(q_pages[2][:], 0.0)
        for t in range(PACK):
            if t in (0, 2):
                nc.scalar.copy(p_src[t + 1], p_banks[t + 1][:])
            nc.scalar.copy(q_src[t], q_banks[t][:])

        y = tile("y", PACK * J, F32)
        y_rounded = tile("y_rounded", PACK * J, BF16)
        y_codes = tile("y_codes", J, U32)
        y_scales = tile("y_scales", J, U8)
        out_rows = out_0.rearrange("(p t) j -> p t j", t=PACK)
        out_words = out_1[0].rearrange("p c r -> p (c r)").bitcast(I32)

        def round_pair(copy, t, cols):
            copy(
                y_rounded[:].rearrange("p (j t) -> p j t", t=PACK)[:, cols, t : t + 2],
                y[:].rearrange("p (t j) -> p j t", t=PACK)[:, cols, t : t + 2],
            )

        def add_pages(engine, t, cols):
            dst = y[:, t * J + cols.start : t * J + cols.stop]
            engine.tensor_tensor(dst, p_pages[t % 3][:, cols], q_pages[t % 3][:, cols], ADD)
            nc.sync.dma_start(out_rows[:, t, cols], dst)

        def add_pages_turned(t):
            blocks = [slice(b * P, (b + 1) * P) for b in range(BANK // P)]
            turned = []
            for h in range(HALVES):
                summed = bank((0, 4, 6)[t] + h)
                for blk in blocks:
                    cols = slice(h * BANK + blk.start, h * BANK + blk.stop)
                    for first, page in ((True, p_pages[t % 3]), (False, q_pages[t % 3])):
                        nc.tensor.matmul(
                            summed[:, blk], page[:, cols], ident[:], start=first, stop=not first, is_transpose=True
                        )
                turned.append(y[:, 3 * J + h * BANK : 3 * J + (h + 1) * BANK])
                nc.scalar.copy(turned[h], summed[:])
            for h in range(HALVES):
                back = bank((2, 6, 0)[t] + h)
                for blk in blocks:
                    nc.tensor.transpose(back[:, blk], turned[h][:, blk], ident[:])
                nc.scalar.copy(y[:, t * J + h * BANK : t * J + (h + 1) * BANK], back[:])
            nc.scalar.dma_start(out_rows[:, t, :], y[:, t * J : (t + 1) * J])

        nc.vector.tensor_copy(p_pages[1][:].indirect(list2[:]), p_src[1])
        for t in range(PACK):
            if t >= 2:
                nc.vector.tensor_copy(p_pages[t % 3][:].indirect(list2[:]), p_src[t])
            nc.vector.tensor_copy(q_pages[t % 3][:].indirect(list3[:]), q_src[t])
            if t == 0:
                nc.scalar.copy(p_src[2], p_banks[2][:])
            if t < 3:
                add_pages_turned(t)
            if t == 1:
                round_pair(nc.scalar.copy, 0, slice(0, J))

        first, second = slice(0, BANK), slice(BANK, J)
        add_pages(nc.vector, PACK - 1, first)
        add_pages(nc.vector, PACK - 1, second)
        round_pair(nc.scalar.copy, 2, first)
        round_pair(nc.vector.tensor_copy, 2, second)
        for cols in (second, first):
            nc.vector.quantize_mx(
                out=y_codes[:, cols].bitcast(FP8X4),
                scales=y_scales[:, cols],
                in_=y_rounded[:, PACK * cols.start : PACK * cols.stop],
            )
            nc.sync.dma_start(out_words[:, cols], y_codes[:, cols].bitcast(I32))
        for q in range(4):
            nc.scalar.dma_start(
                out_2[0, 4 * q : 4 * q + 4, :].bitcast(I32), y_scales[32 * q : 32 * q + 4, :].bitcast(I32)
            )
